import numpy as np
import ml_dtypes


def mxq(x, axis, fmt="e4m3"):
    dtype, down = {"e4m3": (ml_dtypes.float8_e4m3fn, 7), "e5m2": (ml_dtypes.float8_e5m2, 14)}[fmt]
    v = np.moveaxis(np.asarray(x, np.float32).astype(ml_dtypes.bfloat16).astype(np.float64), axis, -1)
    blocks = v.reshape(v.shape[:-1] + (-1, 32))
    amax = np.abs(blocks).max(-1, keepdims=True)
    byte = np.maximum(np.where(amax > 0, np.frexp(amax)[1] - 1 + 127, 0) - down, 1)
    scale = np.exp2(byte - 127.0)
    codes = (blocks / scale).astype(np.float32).astype(dtype).astype(np.float64)
    return np.moveaxis((codes * scale).reshape(v.shape), -1, axis)


WIDE = False


def mx_kscale(k):
    if not WIDE:
        return np.ones(k)
    levels = np.array([10, -10, 5, -5, 0])
    if k % 512:
        return np.exp2(np.random.permutation(np.resize(levels, k // 32))).repeat(32)
    a = np.empty((k // 512, 16))
    for p in range(k // 512):
        a[p, :8] = np.random.permutation(np.resize(levels, 8))
        for g in range(8):
            far = levels[np.abs(levels - a[p, g]) >= 10]
            a[p, g + 8] = far[np.random.randint(len(far))]
    return np.exp2(a.ravel()).repeat(32)


def f64(x):
    return np.asarray(x).astype(np.float64)


def striped(idx):
    return np.tile(idx.reshape(-1, 16).T, (8, 1)).astype(np.uint16)


def unstriped(offs):
    return offs[:16].T.reshape(-1).astype(np.int64)


def pack_weight(w):
    k, n = w.shape
    w = f64(np.asarray(w, np.float32).astype(ml_dtypes.bfloat16)).reshape(k // 32, 32, n)
    amax = np.abs(w).max(1)
    byte = np.clip(np.where(amax > 0, np.frexp(amax)[1] - 1 + 127 - 7, 1), 1, 254)
    scaled = (w * np.exp2(127.0 - byte)[:, None, :]).reshape(k, n).astype(np.float32)
    words = np.ascontiguousarray(scaled.reshape(k // 512, 128, 4, n).transpose(0, 1, 3, 2)).astype(ml_dtypes.float8_e4m3fn).view(np.uint8)
    return words, np.ascontiguousarray(byte.astype(np.uint8).reshape(k // 512, 16, n))


def unpack_weight(words, scales):
    g, p, n, _ = words.shape
    vals = np.ascontiguousarray(words).view(ml_dtypes.float8_e4m3fn).astype(np.float64) * np.repeat(np.exp2(scales.astype(np.float64) - 127.0), 8, axis=1)[..., None]
    return vals.transpose(0, 1, 3, 2).reshape(g * 512, n)


def relu(v):
    return np.maximum(v, 0.0)


K, T, E, C, N = 1024, 1024, 8, 256, 128


def by_expert(wq, xq):
    return np.concatenate([wq[e].T @ xq[:, e * C:(e + 1) * C] for e in range(E)], axis=1)


def setup_inputs():
    n = np.random.standard_normal
    s = mx_kscale(K)[:, None]
    first = np.random.permutation(np.repeat(np.arange(E), T // E))
    second = (first + 1 + np.random.permutation(np.repeat(np.arange(E - 1), -(-T // (E - 1)))[:T])) % E
    while np.bincount(second, minlength=E).max() != T // E:
        load = np.bincount(second, minlength=E); hi, lo = int(load.argmax()), int(load.argmin())
        t = np.flatnonzero((second == hi) & (first != lo))[0]; second[t] = lo
    slot_token = np.empty(E * C, np.int64); pos = np.empty((2, T), np.int64); fill = np.zeros(E, np.int64)
    place = np.stack([np.random.permutation(C) for _ in range(E)])
    for r, deal in enumerate((first, second)):
        for t in np.random.permutation(T):
            e = deal[t]; j = e * C + place[e, fill[e]]; fill[e] += 1; slot_token[j] = t; pos[r, t] = j
    g = np.random.uniform(0.2, 0.8, T)
    packed = [pack_weight(m) for m in n((E, K, N)) / np.sqrt(K) / s[None]]
    return {
        "xT": (n((K, T)) * s).astype(np.float32),
        "w_words": np.stack([m[0] for m in packed]),
        "w_scales": np.stack([m[1] for m in packed]),
        "b": (0.3 * n((N, E))).astype(np.float32),
        "gate": np.stack([np.tile(g, (N, 1)), np.tile(1.0 - g, (N, 1))]).astype(np.float32),
        "offs": striped(slot_token),
        "pos1": striped(pos[0]),
        "pos2": striped(pos[1]),
    }


def reference(xT, w_words, w_scales, b, gate, offs, pos1, pos2):
    idx = unstriped(offs)
    xq = mxq(f64(xT)[:, idx], 0, "e4m3")
    w = np.stack([unpack_weight(w_words[e], w_scales[e]) for e in range(E)])
    y = by_expert(w, xq)
    y = relu(y + np.repeat(f64(b), C, axis=1))
    return f64(gate[0]) * y[:, unstriped(pos1)] + f64(gate[1]) * y[:, unstriped(pos2)]

@@ -1,0 +1,141 @@
+from contextlib import ExitStack
+
+import concourse.mybir as mybir
+
+K, T, E, C, N = 1024, 1024, 8, 256, 128
+SLOTS = E * C
+FLOPS = 2 * K * N * SLOTS
+
+F32 = mybir.dt.float32
+BF16 = mybir.dt.bfloat16
+I32 = mybir.dt.int32
+U32 = mybir.dt.uint32
+U16 = mybir.dt.uint16
+U8 = mybir.dt.uint8
+FP8X4 = mybir.dt.float8_e4m3fn_x4
+MULT = mybir.AluOpType.mult
+ADD = mybir.AluOpType.add
+MAX = mybir.AluOpType.max
+RELU = mybir.ActivationFunctionType.Relu
+
+P = 128
+PACK = 4
+PASSES = K // (P * PACK)
+
+CHUNKS = (
+    ((0, 512, 256), (512, 256, 128), (768, 256, 128)),
+    ((0, 512, 0), (512, 256, 0), (768, 256, 0)),
+)
+WORD_CUTS = (((0, 768), (768, 768), (1536, 512)), ((0, 768), (768, 768), (1536, 256), (1792, 256)))
+BYTE_CUTS = ((0, 768), (768, 768), (1536, 512))
+OUT_CUTS = ((0, 512), (512, 256), (768, 256))
+
+
+def tile_routed_moe_kernel(tc, xT, w_words, w_scales, b, gate, offs, pos1, pos2, out):
+    nc = tc.nc
+    with ExitStack() as ctx:
+        keep = ctx.enter_context(tc.tile_pool(name="keep", bufs=1))
+        psum = ctx.enter_context(tc.psum_pool(name="psum", bufs=1))
+
+        offs_t = keep.tile([P, SLOTS // 16], U16, name="offs_t")
+        pos1_t = keep.tile([P, T // 16], U16, name="pos1_t")
+        pos2_t = keep.tile([P, T // 16], U16, name="pos2_t")
+        x_scales = keep.tile([P, T], U8, name="x_scales", align_bytes=64)
+        w_sc = keep.tile([P, E * PASSES, N], U8, name="w_sc", align_bytes=64)
+        nc.gpsimd.memset(x_scales[:], 0)
+        nc.vector.memset(w_sc[:].rearrange("p g n -> p (g n)").bitcast(I32), 0)
+
+        nc.sync.dma_start(offs_t[:], offs)
+        xv = xT.rearrange("(a p t) n -> a p t n", p=P, t=PACK)
+        raw = {}
+        for a in range(PASSES):
+            for c0, n, v in CHUNKS[a]:
+                r = keep.tile([P, PACK, n], F32, name=f"raw_{a}_{c0}")
+                nc.sync.dma_start(out=r[:], in_=xv[a, :, :, c0 : c0 + n])
+                raw[a, c0] = r
+        w_q = keep.tile([P, E * PASSES, N * PACK], U8, name="w_q", align_bytes=64)
+        nc.sync.dma_start(out=w_q[:], in_=w_words.rearrange("e a p n r -> p (e a) (n r)"))
+        sc_rows = w_scales.rearrange("e a q n -> q (e a) n")
+        for q in range(4):
+            nc.sync.dma_start(
+                out=w_sc[32 * q : 32 * q + 4].bitcast(I32),
+                in_=sc_rows[4 * q : 4 * q + 4].bitcast(I32),
+            )
+        b_t = keep.tile([P, E], F32, name="b_t")
+        nc.sync.dma_start(out=b_t[:], in_=b)
+        nc.sync.dma_start(pos1_t[:], pos1)
+        nc.sync.dma_start(pos2_t[:], pos2)
+        g = []
+        for i in range(2):
+            gt = keep.tile([P, T], F32, name=f"gate_{i}")
+            nc.sync.dma_start(out=gt[:], in_=gate[i])
+            g.append(gt)
+
+        codes = []
+        words = []
+        for a in range(PASSES):
+            codes.append(keep.tile([P, T], U32, name=f"codes_{a}", align_bytes=64))
+            words.append(keep.tile([P, SLOTS], U32, name=f"words_{a}", align_bytes=64))
+        scales = keep.tile([P, SLOTS], U8, name="scales", align_bytes=64)
+        y = keep.tile([P, SLOTS], F32, name="y")
+
+        def interleave(a):
+            parts = []
+            for c0, n, v in CHUNKS[a]:
+                r = raw[a, c0]
+                for lo, hi, eng in ((0, v, "v"), (v, n, "s")):
+                    if hi > lo:
+                        gt = keep.tile([P, hi - lo, PACK], BF16, name=f"grouped_{a}_{c0 + lo}", align_bytes=64)
+                        dst = gt[:].rearrange("p (c i) t -> p c t i", i=4)
+                        src = r[:, :, lo:hi].rearrange("p t (c i) -> p c t i", i=4)
+                        if eng == "v":
+                            nc.vector.tensor_copy(out=dst, in_=src)
+                        else:
+                            nc.scalar.copy(out=dst, in_=src)
+                        parts.append((c0 + lo, c0 + hi, gt))
+            return parts
+
+        def quantise(a, parts):
+            for lo, hi, gt in parts:
+                nc.vector.quantize_mx(
+                    out=codes[a][:, lo:hi].bitcast(FP8X4),
+                    scales=x_scales[4 * a : P, lo:hi],
+                    in_=gt[:].rearrange("p n t -> p (n t)"),
+                )
+
+        def gather(dst, window, cut):
+            s0, n = cut
+            nc.vector.tensor_copy(dst[:, s0 : s0 + n], window[:].indirect(offs_t[:, s0 // 16 : (s0 + n) // 16]))
+
+        quantise(0, interleave(0))
+        for cut in WORD_CUTS[0]:
+            gather(words[0], codes[0], cut)
+        quantise(1, interleave(1))
+        for cut in BYTE_CUTS:
+            gather(scales, x_scales, cut)
+        for cut in WORD_CUTS[1]:
+            gather(words[1], codes[1], cut)
+            for e in range(cut[0] // C, (cut[0] + cut[1]) // C):
+                cols = slice(e * C, (e + 1) * C)
+                acc = psum.tile([P, C], F32, name=f"acc_{e}")
+                for a in range(PASSES):
+                    nc.tensor.matmul_mx(
+                        out=acc[:],
+                        lhsT=w_q[:, e * PASSES + a, :].bitcast(FP8X4),
+                        lhsT_scale=w_sc[:, e * PASSES + a, :],
+                        rhs=words[a][:, cols].bitcast(FP8X4),
+                        rhs_scale=scales[4 * a : P, cols],
+                        start=(a == 0),
+                        stop=(a == PASSES - 1),
+                    )
+                nc.scalar.activation(y[:, cols], acc[:], RELU, bias=b_t[:, e : e + 1])
+
+        m1 = keep.tile([P, T], F32, name="m1")
+        m2 = keep.tile([P, T], F32, name="m2")
+        o = keep.tile([P, T], F32, name="o")
+        nc.vector.tensor_tensor(m1[:], y[:].indirect(pos1_t[:]), g[0][:], MULT)
+        for t0, n in OUT_CUTS:
+            cols = slice(t0, t0 + n)
+            nc.vector.tensor_tensor(m2[:, cols], y[:].indirect(pos2_t[:, t0 // 16 : (t0 + n) // 16]), g[1][:, cols], MULT)
+            nc.vector.tensor_tensor(o[:, cols], m1[:, cols], m2[:, cols], ADD)
+            nc.sync.dma_start(out=out[:, cols], in_=o[:, cols])

@@ -22,9 +22,10 @@ P = 128
 PACK = 4
 PASSES = K // (P * PACK)
 
-CHUNKS = (
-    ((0, 512, 256), (512, 256, 128), (768, 256, 128)),
-    ((0, 512, 0), (512, 256, 0), (768, 256, 0)),
+LOADS = (((0, 512), (512, 256), (768, 256)), ((0, 256), (256, 256), (512, 256), (768, 256)))
+PIECES = (
+    ((0, 256, 256), (256, 256, 0), (512, 256, 160), (768, 256, 160)),
+    ((0, 256, 0), (256, 256, 0), (512, 256, 0), (768, 256, 0)),
 )
 WORD_CUTS = (((0, 768), (768, 768), (1536, 512)), ((0, 768), (768, 768), (1536, 256), (1792, 256)))
 BYTE_CUTS = ((0, 768), (768, 768), (1536, 512))
@@ -45,14 +46,15 @@ def tile_routed_moe_kernel(tc, xT, w_words, w_scales, b, gate, offs, pos1, pos2,
         nc.gpsimd.memset(x_scales[:], 0)
         nc.vector.memset(w_sc[:].rearrange("p g n -> p (g n)").bitcast(I32), 0)
 
-        nc.sync.dma_start(offs_t[:], offs)
         xv = xT.rearrange("(a p t) n -> a p t n", p=P, t=PACK)
         raw = {}
         for a in range(PASSES):
-            for c0, n, v in CHUNKS[a]:
+            for c0, n in LOADS[a]:
                 r = keep.tile([P, PACK, n], F32, name=f"raw_{a}_{c0}")
                 nc.sync.dma_start(out=r[:], in_=xv[a, :, :, c0 : c0 + n])
                 raw[a, c0] = r
+            if a == 0:
+                nc.sync.dma_start(offs_t[:], offs)
         w_q = keep.tile([P, E * PASSES, N * PACK], U8, name="w_q", align_bytes=64)
         nc.sync.dma_start(out=w_q[:], in_=w_words.rearrange("e a p n r -> p (e a) (n r)"))
         sc_rows = w_scales.rearrange("e a q n -> q (e a) n")
@@ -79,56 +81,64 @@ def tile_routed_moe_kernel(tc, xT, w_words, w_scales, b, gate, offs, pos1, pos2,
         scales = keep.tile([P, SLOTS], U8, name="scales", align_bytes=64)
         y = keep.tile([P, SLOTS], F32, name="y")
 
-        def interleave(a):
-            parts = []
-            for c0, n, v in CHUNKS[a]:
-                r = raw[a, c0]
-                for lo, hi, eng in ((0, v, "v"), (v, n, "s")):
-                    if hi > lo:
-                        gt = keep.tile([P, hi - lo, PACK], BF16, name=f"grouped_{a}_{c0 + lo}", align_bytes=64)
-                        dst = gt[:].rearrange("p (c i) t -> p c t i", i=4)
-                        src = r[:, :, lo:hi].rearrange("p t (c i) -> p c t i", i=4)
-                        if eng == "v":
-                            nc.vector.tensor_copy(out=dst, in_=src)
-                        else:
-                            nc.scalar.copy(out=dst, in_=src)
-                        parts.append((c0 + lo, c0 + hi, gt))
-            return parts
+        def interleave(a, piece):
+            c0, n, v = piece
+            l0 = max(l for l, m in LOADS[a] if l <= c0)
+            r = raw[a, l0]
+            gt = keep.tile([P, n, PACK], BF16, name=f"grouped_{a}_{c0}", align_bytes=64)
+            for lo, hi in ((0, v), (v, n)):
+                if hi > lo:
+                    dst = gt[:, lo:hi, :].rearrange("p (c i) t -> p c t i", i=4)
+                    src = r[:, :, c0 - l0 + lo : c0 - l0 + hi].rearrange("p t (c i) -> p c t i", i=4)
+                    if lo < v:
+                        nc.vector.tensor_copy(out=dst, in_=src)
+                    else:
+                        nc.scalar.copy(out=dst, in_=src)
+            return (c0, n, gt)
 
-        def quantise(a, parts):
-            for lo, hi, gt in parts:
-                nc.vector.quantize_mx(
-                    out=codes[a][:, lo:hi].bitcast(FP8X4),
-                    scales=x_scales[4 * a : P, lo:hi],
-                    in_=gt[:].rearrange("p n t -> p (n t)"),
-                )
+        def quantise(a, part):
+            c0, n, gt = part
+            nc.vector.quantize_mx(
+                out=codes[a][:, c0 : c0 + n].bitcast(FP8X4),
+                scales=x_scales[4 * a : P, c0 : c0 + n],
+                in_=gt[:].rearrange("p n t -> p (n t)"),
+            )
 
         def gather(dst, window, cut):
             s0, n = cut
             nc.vector.tensor_copy(dst[:, s0 : s0 + n], window[:].indirect(offs_t[:, s0 // 16 : (s0 + n) // 16]))
 
-        quantise(0, interleave(0))
-        for cut in WORD_CUTS[0]:
-            gather(words[0], codes[0], cut)
-        quantise(1, interleave(1))
-        for cut in BYTE_CUTS:
+        def product(acc, a, col, n):
+            e = col // C
+            nc.tensor.matmul_mx(
+                out=acc[:],
+                lhsT=w_q[:, e * PASSES + a, :].bitcast(FP8X4),
+                lhsT_scale=w_sc[:, e * PASSES + a, :],
+                rhs=words[a][:, col : col + n].bitcast(FP8X4),
+                rhs_scale=scales[4 * a : P, col : col + n],
+                start=(a == 0),
+                stop=(a == PASSES - 1),
+            )
+
+        for a in range(PASSES):
+            for part in [interleave(a, piece) for piece in PIECES[a]]:
+                quantise(a, part)
+            if a == 0:
+                for cut in WORD_CUTS[0]:
+                    gather(words[0], codes[0], cut)
+
+        accs = []
+        for i, cut in enumerate(BYTE_CUTS):
             gather(scales, x_scales, cut)
+            for e in range(cut[0] // C, (cut[0] + cut[1]) // C):
+                acc = psum.tile([P, C], F32, name=f"acc_{e}")
+                product(acc, 0, e * C, C)
+                accs.append(acc)
         for cut in WORD_CUTS[1]:
             gather(words[1], codes[1], cut)
             for e in range(cut[0] // C, (cut[0] + cut[1]) // C):
-                cols = slice(e * C, (e + 1) * C)
-                acc = psum.tile([P, C], F32, name=f"acc_{e}")
-                for a in range(PASSES):
-                    nc.tensor.matmul_mx(
-                        out=acc[:],
-                        lhsT=w_q[:, e * PASSES + a, :].bitcast(FP8X4),
-                        lhsT_scale=w_sc[:, e * PASSES + a, :],
-                        rhs=words[a][:, cols].bitcast(FP8X4),
-                        rhs_scale=scales[4 * a : P, cols],
-                        start=(a == 0),
-                        stop=(a == PASSES - 1),
-                    )
-                nc.scalar.activation(y[:, cols], acc[:], RELU, bias=b_t[:, e : e + 1])
+                product(accs[e], 1, e * C, C)
+                nc.scalar.activation(y[:, e * C : (e + 1) * C], accs[e][:], RELU, bias=b_t[:, e : e + 1])
 
         m1 = keep.tile([P, T], F32, name="m1")
         m2 = keep.tile([P, T], F32, name="m2")

@@ -1,6 +1,7 @@
 from contextlib import ExitStack
 
 import concourse.mybir as mybir
+from concourse.masks import make_identity
 
 K, T, E, C, N = 1024, 1024, 8, 256, 128
 SLOTS = E * C
@@ -24,12 +25,12 @@ PASSES = K // (P * PACK)
 
 LOADS = (((0, 512), (512, 256), (768, 256)), ((0, 256), (256, 256), (512, 256), (768, 256)))
 PIECES = (
-    ((0, 256, 256), (256, 256, 0), (512, 256, 160), (768, 256, 160)),
+    ((0, 256, 256), (256, 256, 0), (512, 256, 160), (768, 256, 192)),
     ((0, 256, 0), (256, 256, 0), (512, 256, 0), (768, 256, 0)),
 )
 WORD_CUTS = (((0, 768), (768, 768), (1536, 512)), ((0, 768), (768, 768), (1536, 256), (1792, 256)))
 BYTE_CUTS = ((0, 768), (768, 768), (1536, 512))
-OUT_CUTS = ((0, 512), (512, 256), (768, 256))
+OUT_CUTS = ((256, 512), (768, 256))
 
 
 def tile_routed_moe_kernel(tc, xT, w_words, w_scales, b, gate, offs, pos1, pos2, out):
@@ -45,6 +46,9 @@ def tile_routed_moe_kernel(tc, xT, w_words, w_scales, b, gate, offs, pos1, pos2,
         w_sc = keep.tile([P, E * PASSES, N], U8, name="w_sc", align_bytes=64)
         nc.gpsimd.memset(x_scales[:], 0)
         nc.vector.memset(w_sc[:].rearrange("p g n -> p (g n)").bitcast(I32), 0)
+
+        ident = keep.tile([P, P], F32, name="ident")
+        make_identity(nc, ident[:])
 
         xv = xT.rearrange("(a p t) n -> a p t n", p=P, t=PACK)
         raw = {}
@@ -127,25 +131,50 @@ def tile_routed_moe_kernel(tc, xT, w_words, w_scales, b, gate, offs, pos1, pos2,
                 for cut in WORD_CUTS[0]:
                     gather(words[0], codes[0], cut)
 
-        accs = []
-        for i, cut in enumerate(BYTE_CUTS):
+        units = [(e * C, C) for e in range(E)]
+
+        def scaled_sum(i):
+            lo, n = units[i]
+            acc = psum.tile([P, n], F32, name=f"acc_{i}", tag=f"bank_{i % 8}")
+            return acc
+
+        accs = {}
+        for cut in BYTE_CUTS:
             gather(scales, x_scales, cut)
-            for e in range(cut[0] // C, (cut[0] + cut[1]) // C):
-                acc = psum.tile([P, C], F32, name=f"acc_{e}")
-                product(acc, 0, e * C, C)
-                accs.append(acc)
+            for i, (lo, n) in enumerate(units):
+                if cut[0] <= lo < cut[0] + cut[1] and i < 8:
+                    accs[i] = scaled_sum(i)
+                    product(accs[i], 0, lo, n)
         for cut in WORD_CUTS[1]:
             gather(words[1], codes[1], cut)
-            for e in range(cut[0] // C, (cut[0] + cut[1]) // C):
-                product(accs[e], 1, e * C, C)
-                nc.scalar.activation(y[:, e * C : (e + 1) * C], accs[e][:], RELU, bias=b_t[:, e : e + 1])
+            for i, (lo, n) in enumerate(units):
+                if cut[0] <= lo < cut[0] + cut[1]:
+                    if i not in accs:
+                        accs[i] = scaled_sum(i)
+                        product(accs[i], 0, lo, n)
+                    product(accs[i], 1, lo, n)
+                    e = lo // C
+                    nc.scalar.activation(y[:, lo : lo + n], accs[i][:], RELU, bias=b_t[:, e : e + 1])
 
         m1 = keep.tile([P, T], F32, name="m1")
         m2 = keep.tile([P, T], F32, name="m2")
         o = keep.tile([P, T], F32, name="o")
-        nc.vector.tensor_tensor(m1[:], y[:].indirect(pos1_t[:]), g[0][:], MULT)
+
+        def weighted(dst, r, t0, n):
+            pos = (pos1_t, pos2_t)[r]
+            nc.vector.tensor_tensor(dst[:, t0 : t0 + n], y[:].indirect(pos[:, t0 // 16 : (t0 + n) // 16]), g[r][:, t0 : t0 + n], MULT)
+
+        n0 = 256
+        both = psum.tile([P, n0], F32, name="both", tag="bank_1")
+        weighted(m1, 0, 0, n0)
+        nc.tensor.matmul(both[:], ident[:], m1[:, :n0], start=True, stop=False)
+        weighted(m2, 1, 0, n0)
+        nc.tensor.matmul(both[:], ident[:], m2[:, :n0], start=False, stop=True)
+        nc.scalar.copy(out=o[:, :n0], in_=both[:])
+        nc.sync.dma_start(out=out[:, :n0], in_=o[:, :n0])
+        weighted(m1, 0, n0, T - n0)
         for t0, n in OUT_CUTS:
             cols = slice(t0, t0 + n)
-            nc.vector.tensor_tensor(m2[:, cols], y[:].indirect(pos2_t[:, t0 // 16 : (t0 + n) // 16]), g[1][:, cols], MULT)
+            weighted(m2, 1, t0, n)
             nc.vector.tensor_tensor(o[:, cols], m1[:, cols], m2[:, cols], ADD)
             nc.sync.dma_start(out=out[:, cols], in_=o[:, cols])

@@ -30,7 +30,7 @@ PIECES = (
 )
 WORD_CUTS = (((0, 768), (768, 768), (1536, 512)), ((0, 768), (768, 768), (1536, 256), (1792, 256)))
 BYTE_CUTS = ((0, 768), (768, 768), (1536, 512))
-OUT_CUTS = ((256, 512), (768, 256))
+OUT_CUTS = ((320, 512), (832, 192))
 
 
 def tile_routed_moe_kernel(tc, xT, w_words, w_scales, b, gate, offs, pos1, pos2, out):
@@ -164,7 +164,7 @@ def tile_routed_moe_kernel(tc, xT, w_words, w_scales, b, gate, offs, pos1, pos2,
             pos = (pos1_t, pos2_t)[r]
             nc.vector.tensor_tensor(dst[:, t0 : t0 + n], y[:].indirect(pos[:, t0 // 16 : (t0 + n) // 16]), g[r][:, t0 : t0 + n], MULT)
 
-        n0 = 256
+        n0 = 320
         both = psum.tile([P, n0], F32, name="both", tag="bank_1")
         weighted(m1, 0, 0, n0)
         nc.tensor.matmul(both[:], ident[:], m1[:, :n0], start=True, stop=False)
@@ -172,9 +172,14 @@ def tile_routed_moe_kernel(tc, xT, w_words, w_scales, b, gate, offs, pos1, pos2,
         nc.tensor.matmul(both[:], ident[:], m2[:, :n0], start=False, stop=True)
         nc.scalar.copy(out=o[:, :n0], in_=both[:])
         nc.sync.dma_start(out=out[:, :n0], in_=o[:, :n0])
-        weighted(m1, 0, n0, T - n0)
-        for t0, n in OUT_CUTS:
+        for i, (t0, n) in enumerate(OUT_CUTS):
+            if i == 0:
+                weighted(m1, 0, t0, n)
+                weighted(m2, 1, t0, n)
+            if i + 1 < len(OUT_CUTS):
+                weighted(m1, 0, *OUT_CUTS[i + 1])
             cols = slice(t0, t0 + n)
-            weighted(m2, 1, t0, n)
             nc.vector.tensor_tensor(o[:, cols], m1[:, cols], m2[:, cols], ADD)
             nc.sync.dma_start(out=out[:, cols], in_=o[:, cols])
+            if i + 1 < len(OUT_CUTS):
+                weighted(m2, 1, *OUT_CUTS[i + 1])

from contextlib import ExitStack

import concourse.mybir as mybir
from concourse.masks import make_identity

K, T, E, C, N = 1024, 1024, 8, 256, 128
SLOTS = E * C
FLOPS = 2 * K * N * SLOTS

F32 = mybir.dt.float32
BF16 = mybir.dt.bfloat16
I32 = mybir.dt.int32
U32 = mybir.dt.uint32
U16 = mybir.dt.uint16
U8 = mybir.dt.uint8
FP8X4 = mybir.dt.float8_e4m3fn_x4
MULT = mybir.AluOpType.mult
ADD = mybir.AluOpType.add
MAX = mybir.AluOpType.max
RELU = mybir.ActivationFunctionType.Relu

P = 128
PACK = 4
PASSES = K // (P * PACK)

LOADS = (((0, 512), (512, 256), (768, 256)), ((0, 256), (256, 256), (512, 256), (768, 256)))
PIECES = (
    ((0, 256, 256), (256, 256, 0), (512, 256, 160), (768, 256, 192)),
    ((0, 256, 0), (256, 256, 0), (512, 256, 0), (768, 256, 0)),
)
WORD_CUTS = (((0, 768), (768, 768), (1536, 512)), ((0, 768), (768, 768), (1536, 256), (1792, 256)))
BYTE_CUTS = ((0, 768), (768, 768), (1536, 512))
OUT_CUTS = ((320, 512), (832, 192))


def tile_routed_moe_kernel(tc, xT, w_words, w_scales, b, gate, offs, pos1, pos2, out):
    nc = tc.nc
    with ExitStack() as ctx:
        keep = ctx.enter_context(tc.tile_pool(name="keep", bufs=1))
        psum = ctx.enter_context(tc.psum_pool(name="psum", bufs=1))

        offs_t = keep.tile([P, SLOTS // 16], U16, name="offs_t")
        pos1_t = keep.tile([P, T // 16], U16, name="pos1_t")
        pos2_t = keep.tile([P, T // 16], U16, name="pos2_t")
        x_scales = keep.tile([P, T], U8, name="x_scales", align_bytes=64)
        w_sc = keep.tile([P, E * PASSES, N], U8, name="w_sc", align_bytes=64)
        nc.gpsimd.memset(x_scales[:], 0)
        nc.vector.memset(w_sc[:].rearrange("p g n -> p (g n)").bitcast(I32), 0)

        ident = keep.tile([P, P], F32, name="ident")
        make_identity(nc, ident[:])

        xv = xT.rearrange("(a p t) n -> a p t n", p=P, t=PACK)
        raw = {}
        for a in range(PASSES):
            for c0, n in LOADS[a]:
                r = keep.tile([P, PACK, n], F32, name=f"raw_{a}_{c0}")
                nc.sync.dma_start(out=r[:], in_=xv[a, :, :, c0 : c0 + n])
                raw[a, c0] = r
            if a == 0:
                nc.sync.dma_start(offs_t[:], offs)
        w_q = keep.tile([P, E * PASSES, N * PACK], U8, name="w_q", align_bytes=64)
        nc.sync.dma_start(out=w_q[:], in_=w_words.rearrange("e a p n r -> p (e a) (n r)"))
        sc_rows = w_scales.rearrange("e a q n -> q (e a) n")
        for q in range(4):
            nc.sync.dma_start(
                out=w_sc[32 * q : 32 * q + 4].bitcast(I32),
                in_=sc_rows[4 * q : 4 * q + 4].bitcast(I32),
            )
        b_t = keep.tile([P, E], F32, name="b_t")
        nc.sync.dma_start(out=b_t[:], in_=b)
        nc.sync.dma_start(pos1_t[:], pos1)
        nc.sync.dma_start(pos2_t[:], pos2)
        g = []
        for i in range(2):
            gt = keep.tile([P, T], F32, name=f"gate_{i}")
            nc.sync.dma_start(out=gt[:], in_=gate[i])
            g.append(gt)

        codes = []
        words = []
        for a in range(PASSES):
            codes.append(keep.tile([P, T], U32, name=f"codes_{a}", align_bytes=64))
            words.append(keep.tile([P, SLOTS], U32, name=f"words_{a}", align_bytes=64))
        scales = keep.tile([P, SLOTS], U8, name="scales", align_bytes=64)
        y = keep.tile([P, SLOTS], F32, name="y")

        def interleave(a, piece):
            c0, n, v = piece
            l0 = max(l for l, m in LOADS[a] if l <= c0)
            r = raw[a, l0]
            gt = keep.tile([P, n, PACK], BF16, name=f"grouped_{a}_{c0}", align_bytes=64)
            for lo, hi in ((0, v), (v, n)):
                if hi > lo:
                    dst = gt[:, lo:hi, :].rearrange("p (c i) t -> p c t i", i=4)
                    src = r[:, :, c0 - l0 + lo : c0 - l0 + hi].rearrange("p t (c i) -> p c t i", i=4)
                    if lo < v:
                        nc.vector.tensor_copy(out=dst, in_=src)
                    else:
                        nc.scalar.copy(out=dst, in_=src)
            return (c0, n, gt)

        def quantise(a, part):
            c0, n, gt = part
            nc.vector.quantize_mx(
                out=codes[a][:, c0 : c0 + n].bitcast(FP8X4),
                scales=x_scales[4 * a : P, c0 : c0 + n],
                in_=gt[:].rearrange("p n t -> p (n t)"),
            )

        def gather(dst, window, cut):
            s0, n = cut
            nc.vector.tensor_copy(dst[:, s0 : s0 + n], window[:].indirect(offs_t[:, s0 // 16 : (s0 + n) // 16]))

        def product(acc, a, col, n):
            e = col // C
            nc.tensor.matmul_mx(
                out=acc[:],
                lhsT=w_q[:, e * PASSES + a, :].bitcast(FP8X4),
                lhsT_scale=w_sc[:, e * PASSES + a, :],
                rhs=words[a][:, col : col + n].bitcast(FP8X4),
                rhs_scale=scales[4 * a : P, col : col + n],
                start=(a == 0),
                stop=(a == PASSES - 1),
            )

        for a in range(PASSES):
            for part in [interleave(a, piece) for piece in PIECES[a]]:
                quantise(a, part)
            if a == 0:
                for cut in WORD_CUTS[0]:
                    gather(words[0], codes[0], cut)

        units = [(e * C, C) for e in range(E)]

        def scaled_sum(i):
            lo, n = units[i]
            acc = psum.tile([P, n], F32, name=f"acc_{i}", tag=f"bank_{i % 8}")
            return acc

        accs = {}
        for cut in BYTE_CUTS:
            gather(scales, x_scales, cut)
            for i, (lo, n) in enumerate(units):
                if cut[0] <= lo < cut[0] + cut[1] and i < 8:
                    accs[i] = scaled_sum(i)
                    product(accs[i], 0, lo, n)
        for cut in WORD_CUTS[1]:
            gather(words[1], codes[1], cut)
            for i, (lo, n) in enumerate(units):
                if cut[0] <= lo < cut[0] + cut[1]:
                    if i not in accs:
                        accs[i] = scaled_sum(i)
                        product(accs[i], 0, lo, n)
                    product(accs[i], 1, lo, n)
                    e = lo // C
                    nc.scalar.activation(y[:, lo : lo + n], accs[i][:], RELU, bias=b_t[:, e : e + 1])

        m1 = keep.tile([P, T], F32, name="m1")
        m2 = keep.tile([P, T], F32, name="m2")
        o = keep.tile([P, T], F32, name="o")

        def weighted(dst, r, t0, n):
            pos = (pos1_t, pos2_t)[r]
            nc.vector.tensor_tensor(dst[:, t0 : t0 + n], y[:].indirect(pos[:, t0 // 16 : (t0 + n) // 16]), g[r][:, t0 : t0 + n], MULT)

        n0 = 320
        both = psum.tile([P, n0], F32, name="both", tag="bank_1")
        weighted(m1, 0, 0, n0)
        nc.tensor.matmul(both[:], ident[:], m1[:, :n0], start=True, stop=False)
        weighted(m2, 1, 0, n0)
        nc.tensor.matmul(both[:], ident[:], m2[:, :n0], start=False, stop=True)
        nc.scalar.copy(out=o[:, :n0], in_=both[:])
        nc.sync.dma_start(out=out[:, :n0], in_=o[:, :n0])
        for i, (t0, n) in enumerate(OUT_CUTS):
            if i == 0:
                weighted(m1, 0, t0, n)
                weighted(m2, 1, t0, n)
            if i + 1 < len(OUT_CUTS):
                weighted(m1, 0, *OUT_CUTS[i + 1])
            cols = slice(t0, t0 + n)
            nc.vector.tensor_tensor(o[:, cols], m1[:, cols], m2[:, cols], ADD)
            nc.sync.dma_start(out=out[:, cols], in_=o[:, cols])
            if i + 1 < len(OUT_CUTS):
                weighted(m2, 1, *OUT_CUTS[i + 1])
